import numpy as np, ml_dtypes
CORES = [3,7,11,15,131,135,139,143]
N = 8
BF = ml_dtypes.bfloat16
W, C, S, RO, B = 2048, 256, 2, 4, 8
def parts(rng):
    x = rng.integers(122, 135, (N, 8, 16, W), dtype=np.int16)
    far = rng.random((N, 8, 16, W), dtype=np.float32) < rng.choice(np.array([0.02, 0.06, 0.1]), (N, 8, 16, 1))
    far = far | (rng.random((N, 8, 1, W)) < 0.02)
    x = np.where(far, rng.integers(0, 256, (N, 8, 16, W), dtype=np.int16), x)
    return x, rng.integers(0, W, (N, 8, 16, C)), rng.integers(0, 4096, (N, 8, 16, 1)), rng.integers(-160, 161, (N, 8, RO, S, C))
def pack(x, c, w, sl):
    return {"xt": np.ascontiguousarray(np.reshape(x, (N, 128, W))).astype(np.float32).astype(BF), "ch": np.ascontiguousarray(np.reshape(c, (N, 128, C))).astype(np.int32),
            "wt": np.ascontiguousarray(np.reshape(w, (N, 128, 1))).astype(np.int32), "sl": np.ascontiguousarray(np.reshape(sl, (N, 8, RO * S * C))).astype(np.int32)}
def setup_inputs(rng):
    return pack(*parts(rng))
def setup_inputs_spread(rng):
    x = np.minimum((np.exp2(8 * rng.random((N, 8, 1, W))) * rng.random((N, 8, 16, W), dtype=np.float32)).astype(np.int16), 255)
    x = np.where(rng.random((N, 8, 16, 1)) < 0.4, 255 - x, x)
    c = np.minimum((W * rng.random((N, 8, 16, C)) ** rng.choice(np.array([0.25, 1.0, 3.0]), (N, 8, 1, C))).astype(np.int64), W - 1)
    w = np.minimum(np.exp2(12 * rng.random((N, 8, 16, 1))).astype(np.int64) - 1, 4095)
    return pack(x, c, w, rng.integers(-255, 256, (N, 8, RO, S, C)))
def setup_inputs_ends(rng):
    b = np.zeros((N, 8, 16, W), bool); sh = int(rng.integers(0, 4))
    for r in range(N):
        for g in range(8):
            md = 4 if g == 7 else (g + r + sh) % 4
            if md == 0: b[r, g] = rng.random((1, W)) < 0.042
            elif md == 1: b[r, g] = rng.random((16, W)) < rng.choice(np.array([0.042, 0.5, 0.958]), (16, 1))
            elif md == 2: b[r, g] = rng.random((1, W)) < 0.958
            elif md == 3: b[r, g] = rng.random((16, W)) < 0.042
            else:
                b[r, g] = rng.random((1, W)) < 0.042; b[r, g, 15] = rng.random(W) < 0.042
    b[:, 7, :, 0] = False; b[:, 7, :, W - 1] = True
    c = np.where(rng.random((N, 8, 16, C)) < rng.choice(np.array([0.0, 0.0625, 0.5, 0.5, 0.9375, 1.0]), (N, 8, 1, C)), W - 1, 0)
    c[:, :, :, 0] = 0; c[:, 7, :, C - 2] = W - 1
    k = np.arange(16); nm = np.where(k % 2 == 0, W - 1, 0); nx = (((nm * 16) >> 6) + nm + 613 * k) & (W - 1)
    c[:, 7, :, C - 1] = nm
    last, first = b[N - 1, 7], b[0, 7]
    last[:, nx] = False; last[:15, nx[0]] = True; last[15, nx] = True
    first[:, nx] = False; first[:, nx[0]] = True
    w = 4095 * rng.integers(0, 2, (N, 8, 16, 1)); w[:, 1, 0] = 0; w[:, 1, 1] = 4095; w[0, 0] = 0; w[N - 1, 7] = 4095
    sl = 510 * rng.integers(0, 2, (N, 8, RO, S, C)) - 255; sl[N - 1, 7, 0, 0, C - 1] = -255
    return pack(255 * b.astype(np.int16), c, w, sl)
def setup_inputs_corners(rng):
    x, c, w, sl = parts(rng); i = np.arange(C)
    x[1, 0] = 255 * rng.integers(0, 2, (16, W))
    pin = 5 * C + int(rng.integers(0, C)) if W == 4096 else -1
    for a, m in ((0, int(rng.choice(np.array([31, 32, 33, 8 * C - 1])))), (2, 8 * C)):
        x[a] = rng.integers(0, 256, (8, 16, 1)); x[a, 7, 15] = 255; x[a, 7, 14] = 0
        ways = np.stack([np.zeros((8, C), np.int64), np.full((8, C), W - 1), np.tile(B * i, (8, 1)), np.tile(B * i + B - 1, (8, 1)), rng.integers(0, W, (8, C))])
        c[a] = np.take_along_axis(ways, rng.integers(0, 5, (1, 8, C)), 0).reshape(8, 1, C)
        o = rng.permutation(8 * C)
        if a == 0: o = o[o != pin]
        h = np.zeros(8 * C, bool); h[o[:m]] = True
        sl[a, :, 0] = -255; sl[a, :, 0, 0] = np.where(h.reshape(8, C), 0, -255)
    if N > 4: x[4, :4] = rng.integers(0, 256, (4, 16, 1))
    c[1, 5] = 0; c[1, 6] = W - 1
    for a in (1, 3):
        sl[a] = rng.choice(np.array([-255, -1, 0, 1, 255]), (8, RO, S, C))
        c[a, :5] = np.where(rng.random((5, 1, C)) < 0.5, B * i + (B - 1) * rng.integers(0, 2, (5, 16, C)), c[a, :5])
    w[:, 1] = 0; w[:, 2] = 4095; w[:, 3, :15] = 0; w[:, 3, 15] = 4095; w[:, 4] = 1
    for g, low in ((0, 0), (6, 4095)):
        v = rng.integers(220, 256, 16); v[14] = 2; v[15] = 1
        z = rng.integers(3500, 4096, 16); z[14] = rng.integers(0, 2048); z[15] = 0
        z[15] = (low - int(np.sum(v * z))) & 4095
        if (int(np.sum(v * z)) >> 12) & 1 == 0: z[14] += 2048
        x[0, g] = v.reshape(16, 1); w[0, g] = z.reshape(16, 1)
    if pin >= 0:
        p = int(rng.integers(0, 16)); x[0, 5, p] = 1; w[0, 5] = 0; w[0, 5, p] = 4075
        first = (((c[0, 5] * 4075) >> 6) + c[0, 5]) & (W - 1)
        c[0, 5] = np.where(first == 2557, 0, c[0, 5]); c[0, 5, :, pin - 5 * C] = 4093; sl[0, 5, 0, 0, pin - 5 * C] = 0
        nx = (2557 + 613 * np.arange(16)) & (W - 1); own = x[1, 5]; own[:, nx] = rng.integers(122, 135, (16, 1))
    return pack(x, c, w, sl)
def setup_inputs_ties(rng):
    x = rng.integers(0, 254, (N, 8, 16, 1), dtype=np.int16) + 2 * (rng.random((N, 8, 16, W), dtype=np.float32) < rng.choice(np.array([0.02, 0.05]), (N, 8, 16, 1))).astype(np.int16)
    c = rng.integers(0, W, (N, 8, 16, C)); few = np.take_along_axis(c, rng.integers(0, 4, (N, 8, 16, C)), 2)
    c = np.where(rng.random((N, 8, 1, C)) < 0.5, few, c); sl = rng.integers(-3, 4, (N, 8, RO, S, C))
    x[0] = rng.integers(0, 256, (8, 16, 1)); x[2, :2] = rng.integers(0, 256, (2, 16, 1)); c[0] = rng.integers(0, W, (8, 1, C))
    x[1, :, 15] = rng.integers(0, 254, (8, 1)) + 2 * (np.arange(W) & 1)
    h = np.zeros(8 * C, bool); h[rng.permutation(8 * C)[:26 + 2 * int(rng.integers(0, 3)) + 32 * int(rng.integers(0, C // 4))]] = True
    sl[0, :, 0] = -1; sl[0, :, 0, 0] = np.where(h.reshape(8, C), 0, -1)
    return pack(x, c, rng.integers(0, 4096, (N, 8, 16, 1)), sl)
def check_inputs(d):
    bad = []
    for k, lo, hi in (("xt", 0, 255), ("ch", 0, W - 1), ("wt", 0, 4095), ("sl", -255, 255)):
        v = np.asarray(d[k]).astype(np.float64)
        if not (np.min(v) >= lo and np.max(v) <= hi): bad.append("range of " + k)
        if not np.all(v == np.floor(v)): bad.append("whole numbers in " + k)
    return bad
def look(tab, c):
    v = np.take_along_axis(tab, c.reshape(8, 1, 16 * C), 2).reshape(8, 16, 16, C)
    y = np.max(v, axis=2).astype(np.int64); m = np.min(v, axis=2).astype(np.int64)
    return y, np.add.reduce(y - m, axis=1)
def reference(xt, ch, wt, sl):
    X = xt.astype(np.float32).astype(np.int32).reshape(N, 8, 16, W); c = ch.astype(np.int64).reshape(N, 8, 16, C)
    w = wt.astype(np.int64).reshape(N, 8, 16, 1); slack = sl.astype(np.int64).reshape(N, 8, RO, S, C)
    kappa = np.zeros(N, np.int64); k613 = (613 * np.arange(16)).reshape(1, 16, 1)
    for t in range(RO):
        states, tops, wrong = [], [], []
        for r in range(N):
            q = (r + 1 + t % (N - 1)) % N
            s = c[r]; y, e = look(X[r], s); eq = look(X[q], s)[1]
            fs, fy = s, y; right = np.ones((8, C), bool)
            for j in range(S):
                u = np.add.reduce(w[r] * y, axis=1) & 4095
                n = (((s * u[:, None, :]) >> 6) + s + k613 + 77 * j + kappa[r]) & (W - 1)
                yn, en = look(X[r], n); qn = look(X[q], n)[1]; a = slack[r, :, t, j]
                guess = en <= e + a; true = en + qn <= e + eq + a
                go = (right & true)[:, None, :]; fs = np.where(go, n, fs); fy = np.where(go, yn, fy)
                right = right & (guess == true)
                on = guess[:, None, :]; s = np.where(on, n, s); y = np.where(on, yn, y); e = np.where(guess, en, e); eq = np.where(guess, qn, eq)
            states.append(fs); tops.append(fy); wrong.append(np.count_nonzero(~right) & 31)
        for r in range(N):
            place = (B * np.arange(C)[None, :] + (np.add.reduce(w[r] * tops[r], axis=1) & (B - 1)))[:, None, :]
            old = np.take_along_axis(X[r], place, 2)
            np.put_along_axis(X[r], place, ((old + tops[r]) >> 1).astype(np.int32), 2)
        c = np.stack(states); kappa = np.array(wrong, np.int64)
    return {"yc": c.reshape(N, 128, C).astype(np.float32), "yx": X.reshape(N, 128, W).astype(np.float32).astype(BF)}

from concourse.mybir import AluOpType, AxisListType, ActivationFunctionType

R, NC, HC = 4, 256, 128
HN = 16 * HC
NG = 6

SCRATCH = {
    "tab0": ("sbuf", [128, 2048], "bfloat16"), "tab1": ("sbuf", [128, 2048], "bfloat16"),
    "mxw": ("sbuf", [128, 7 * HN], "bfloat16"),
    "mno": ("sbuf", [128, 2 * HN], "bfloat16"),
    "pmx": ("sbuf", [128, 4 * HN], "bfloat16"), "pmn": ("sbuf", [128, 4 * HN], "bfloat16"),
    "mkx": ("sbuf", [128, HN], "bfloat16"), "mkn": ("sbuf", [128, HN], "bfloat16"),
    "outl": ("sbuf", [128, R * 3 * NC], "uint16"), "inl": ("sbuf", [128, R * 3 * NC], "uint16"),
    "ro": ("sbuf", [128, R * 48], "float32"), "rin": ("sbuf", [128, R * 48], "float32"),
    "chi": ("sbuf", [128, NC], "int32"), "wti": ("sbuf", [128, 1], "int32"), "sli": ("sbuf", [128, 2048], "int32"),
    "slb": ("sbuf", [128, 2048], "bfloat16"), "al": ("sbuf", [128, 128], "float32"),
    "ones": ("sbuf", [128, 144], "bfloat16"), "blk0": ("sbuf", [128, 144], "bfloat16"), "blk": ("sbuf", [128, 144], "bfloat16"),
    "qo": ("sbuf", [128, 144], "bfloat16"), "qn": ("sbuf", [128, 144], "bfloat16"), "q7": ("sbuf", [128, 144], "bfloat16"),
    "qg": ("sbuf", [128, 144], "bfloat16"),
    "wh": ("sbuf", [128, 128], "bfloat16"), "wl": ("sbuf", [128, 128], "bfloat16"),
    "sm": ("sbuf", [128, 768], "float32"), "smi": ("sbuf", [128, 256], "int32"),
    "rt": ("sbuf", [128, 16], "bfloat16"), "fo": ("sbuf", [128, 48], "uint16"), "so": ("sbuf", [128, 16], "uint16"),
    "fy": ("sbuf", [128, NC], "bfloat16"), "xs": ("sbuf", [128, NC], "int32"), "xh": ("sbuf", [128, NC], "int32"),
    "nx": ("sbuf", [128, NC], "int32"), "ycf": ("sbuf", [128, NC], "float32"),
    "nw0": ("sbuf", [128, 4 * NC], "int32"), "nw1": ("sbuf", [128, 4 * NC], "int32"),
}
for _k in range(NG):
    SCRATCH["gb%d" % _k] = ("sbuf", [128, HN], "bfloat16")
for _h in range(2):
    for _k in ("ua", "ub", "uc", "ud"):
        SCRATCH["%s%d" % (_k, _h)] = ("sbuf", [128, HC], "int32")
for _k in range(8):
    SCRATCH["p%d" % _k] = ("psum", [128, 512], "float32")

DMAS = ["dch", "dwt", "dsl", "dx0", "dx1", "dc0", "dc1", "dc2", "dyx0", "dyx1", "dyc"]
SEMAPHORES = ["qv", "qs", "qt", "qg", "loc"] + DMAS
SEMAPHORES += ["l%d%d%d" % (t, k, h) for t in range(R) for k in range(3) for h in range(2)]
SEMAPHORES += ["r%d%d" % (t, k) for t in range(R) for k in range(2)]


def rank_program(g, core, T, topo):
    rank = T.rank_of(core)
    if rank is None:
        return
    A, F = AluOpType, ActivationFunctionType
    N = len(T.cores)
    eng = {"v": g.vector, "s": g.scalar, "t": g.tensor, "g": g, "y": g.sync}
    count = {"v": 0, "s": 0, "t": 0, "g": 0}
    clock = {q: {} for q in eng}
    acc = {}
    nloc = [0]

    def view(name, lo, hi, step=1, parts=None):
        t = T[name]
        if step == 1:
            ap = t[:, lo:hi] if parts is None else t[0:parts, lo:hi]
        else:
            ap = t[:, lo:hi:step] if parts is None else t[0:parts, lo:hi:step]
        return (ap, name, lo, hi)

    def sub(v, lo, n):
        return view(v[1], v[2] + lo, v[2] + lo + n)

    def ind(win, off):
        return (win[0].indirect(off[0]), win, off)

    def learn(q, ck):
        c = clock[q]
        for s, v in ck.items():
            if c.get(s, 0) < v:
                c[s] = v

    def flat(vs):
        out = []
        for v in vs:
            out += [v[1], v[2]] if len(v) == 3 else [v]
        return out

    def region(v):
        if v[1][0] == "p" and len(v[1]) == 2:
            return v[1], 0, 512, True
        return v[1], v[2], v[3], False

    def before(q, reads, writes):
        need, cks = {}, []
        for vs, w in ((reads, False), (writes, True)):
            for v in flat(vs):
                name, lo, hi, ps = region(v)
                for a in acc.get(name, ()):
                    if a[0] < hi and lo < a[1]:
                        if ps and q == "t" and a[3] == "t":
                            continue
                        if w or a[2] or (ps and a[3] != q):
                            need[a[4]] = max(need.get(a[4], 0), a[5])
                            cks.append((a[4], a[6]))
        for s in sorted(need):
            if clock[q].get(s, 0) < need[s] and not any(o != s and ck.get(s, 0) >= need[s] for o, ck in cks):
                eng[q].wait_ge(T.sem[s], need[s])
                clock[q][s] = need[s]
        for _, ck in cks:
            learn(q, ck)

    def after(q, reads, writes, sem, val):
        ck = dict(clock[q])
        ck[sem] = val
        for vs, w in ((reads, False), (writes, True)):
            for v in flat(vs):
                name, lo, hi, ps = region(v)
                lst = acc.setdefault(name, [])
                if w:
                    lst[:] = [a for a in lst if not (lo <= a[0] and a[1] <= hi) or (ps and a[3] == q and not a[2])]
                lst.append((lo, hi, w, q, sem, val, ck))

    def op(q, call, reads, writes):
        before(q, reads, writes)
        ins = call()
        count[q] += 1
        ins.then_inc(T.sem["q" + q], 1)
        after(q, reads, writes, "q" + q, count[q])

    def dma(q, sem, out, in_, reads, writes):
        before(q, reads, writes)
        eng[q].dma_start(out, in_).then_inc(T.sem[sem], 16)
        after(q, reads, writes, sem, 16)

    def cp(out, in_):
        op("v", lambda: g.vector.tensor_copy(out[0], in_[0]), [in_], [out])

    def tt(out, a, b, o):
        op("v", lambda: g.vector.tensor_tensor(out[0], a[0], b[0], o), [a, b], [out])

    def ts(out, a, s1, o1, s2=None, o2=None):
        col = isinstance(s1, tuple)
        rd = [a, s1] if col else [a]
        x1 = s1[0] if col else s1
        if o2 is None:
            op("v", lambda: g.vector.tensor_scalar(out[0], a[0], x1, None, o1), rd, [out])
        else:
            op("v", lambda: g.vector.tensor_scalar(out[0], a[0], x1, s2, o1, o2), rd, [out])

    def fill(out, c):
        op("v", lambda: g.vector.memset(out[0], c), [], [out])

    def mms(out, pairs, start, stop):
        def call():
            ins = None
            for k, (l, r) in enumerate(pairs):
                ins = g.tensor.matmul(out[0], l[0], r[0], start and k == 0, stop and k == len(pairs) - 1)
            return ins
        rd = [l for l, _ in pairs] + [r for _, r in pairs]
        op("t", call, rd, [out])

    def send(dst, src, land, sem):
        before("g", [src], [])
        d = T.cores[dst]
        es = topo.engines(core, d)[:8]
        rid, pid = topo.addr(d, core)
        g.remote_dma(T[land][:, src[2]:src[3]], src[0], T.sem[sem], T.sem.loc, pid, rid, sum(1 << e for e in es))
        nloc[0] += len(es)

    def landed(src, land, lo, hi, sem):
        n = len(topo.engines(T.cores[src], core)[:8])
        acc.setdefault(land, []).append((lo, hi, True, "x", sem, n, {sem: n}))

    cols, nxt = {}, {"sm": 0, "smi": 0}

    def small(name, n, buf="sm"):
        if name not in cols:
            cols[name] = (buf, nxt[buf])
            nxt[buf] += n + (n & 1)
        b, o = cols[name]
        return view(b, o, o + n)

    def partner(t):
        return (rank + 1 + t % (N - 1)) % N

    def asker(t):
        return (rank - 1 - t % (N - 1)) % N

    def lists(t, k, h=None, buf="outl"):
        lo = (t * 3 + k) * NC
        return view(buf, lo, lo + NC) if h is None else view(buf, lo + h * HC, lo + h * HC + HC)

    def send_list(t, k, h=None):
        send(partner(t), lists(t, k, h), "inl", "l%d%d%d" % (t, k, h or 0))

    def send_spans(t, k):
        lo = t * 48
        send(asker(t), view("ro", lo, lo + 32) if k == 0 else view("ro", lo + 32, lo + 48), "rin", "r%d%d" % (t, k))

    for t in range(R):
        for k in range(3):
            for h in ((None,) if k == 0 else (0, 1)):
                v = lists(t, k, h, "inl")
                landed(asker(t), "inl", v[2], v[3], "l%d%d%d" % (t, k, h or 0))
        landed(partner(t), "rin", t * 48, t * 48 + 32, "r%d0" % t)
        landed(partner(t), "rin", t * 48 + 32, t * 48 + 48, "r%d1" % t)

    def names(t, slot, h=None):
        b, lo = "nw%d" % (t % 2), slot * NC
        return view(b, lo, lo + NC) if h is None else view(b, lo + h * HC, lo + h * HC + HC)

    dma("y", "dch", T.chi[:], T.ch[:], [], [view("chi", 0, NC)])
    dma("s", "dx0", T.tab0[:], T.xt[:], [], [view("tab0", 0, 2048)])
    dma("y", "dwt", T.wti[:], T.wt[:], [], [view("wti", 0, 1)])
    dma("y", "dsl", T.sli[0:8, :], T.sl[:], [], [view("sli", 0, 2048)])
    fill(view("ones", 0, 144), 1.0)
    fill(view("mkx", 0, HN), 1.0)
    fill(view("mkn", 0, HN), 0.0)
    fill(view("mkx", 0, HN, 16), 0.0)
    fill(view("mkn", 0, HN, 16), 512.0)
    cp(lists(0, 0), view("chi", 0, NC))
    cp(names(0, 0), view("chi", 0, NC))

    pidx, ic, pm = small("pidx", 8, "smi"), small("ic", 8, "smi"), small("pm", 16, "smi")
    ones, blk = view("ones", 0, 144), view("blk", 0, 144)
    op("g", lambda: g.affine_select(T.blk0[:], T.ones[:], [[-16, 9], [0, 16]], A.is_ge, 0.0, 0, 1), [ones], [view("blk0", 0, 144)])
    op("g", lambda: g.affine_select(T.blk[:], T.blk0[:], [[16, 9], [0, 16]], A.is_ge, 0.0, 15, -1), [view("blk0", 0, 144)], [blk])
    op("g", lambda: g.affine_select(T.qo[:], T.blk[:], [[0, 9], [1, 16]], A.is_equal, 0.0, -15, 0), [blk], [view("qo", 0, 144)])
    op("g", lambda: g.iota(pidx[0], [[0, 8]], 0, 1), [], [pidx])
    op("g", lambda: g.iota(ic[0], [[16, 8]], 0, 0), [], [ic])
    op("g", lambda: g.affine_select(T.qg[:], T.ones[:], [[1, 144]], A.is_equal, 0.0, -15, -16), [ones], [view("qg", 0, 144)])
    send_list(0, 0)

    wti = view("wti", 0, 1)
    for mask, col, src, dst, n in ((4032, "fa", "blk", "wh", 128), (63, "fb", "blk", "wl", 128), (7, "fc", "qo", "q7", 144)):
        i = small(col + "i", 1, "smi")
        f = small(col, 1)
        ts(i, wti, mask, A.bitwise_and)
        cp(f, i)
        ts(view(dst, 0, n), view(src, 0, n), f, A.mult)
    ts(view("qn", 0, 144), view("qo", 0, 144), -1.0, A.mult)
    ts(sub(pm, 0, 8), pidx, 15, A.bitwise_and)
    ib, cb, base, d2, tmp, fl = (small(n, 48) for n in ("ib", "cb", "base", "d2", "tmp", "fl"))
    inn, iv, inq = sub(ib, 0, 16), small("iv", 16), small("inq", 16)
    tt(sub(inn, 0, 8), sub(pm, 0, 8), ic, A.add)
    ts(sub(inn, 8, 8), sub(inn, 0, 8), float(HC), A.add)
    ts(sub(ib, 16, 16), inn, 16.0, A.mult, 15.0, A.add)
    ts(sub(cb, 16, 16), inn, 16.0, A.mult, 15.0 + 4 * HN, A.add)
    ts(iv, inn, 8.0, A.mult)
    ts(inq, inn, 3.0 * NC, A.add, 1.0 / NC, A.mult)
    k6, k613, c0 = small("k6", 2, "smi"), small("k613", 1), small("c0", 1)
    ts(sub(k6, 0, 1), sub(pm, 0, 1), 613.0, A.mult)
    ts(sub(k6, 1, 1), sub(k6, 0, 1), 2047, A.bitwise_and)
    cp(k613, sub(k6, 1, 1))
    cp(c0, sub(k6, 1, 1))
    for t in range(2):
        fill(names(t, 2), 0)

    op("v", lambda: g.vector.tensor_copy(T.slb[0:8, :], T.sli[0:8, :]), [view("sli", 0, 2048)], [view("slb", 0, 2048)])
    mms(view("p7", 0, 128), [(view("qg", 15 - j, 143 - j, 1, 8), view("slb", j, 2048, 16, 8)) for j in range(16)], True, True)

    ring, where = [0], {}

    def gather(key, t, off, chunks=1):
        b = "gb%d" % (ring[0] % NG)
        ring[0] += 1
        w = HC // chunks
        for c in range(chunks):
            src = ind(view("tab%d" % (t % 2), 0, 2048), sub(off, c * w, w))
            dst = view(b, c * w * 16, (c + 1) * w * 16)
            op("s", lambda: g.scalar.activation(dst[0], src[0], F.Copy), [src], [dst])
        where[key] = (b, chunks)

    def scan(key, out, least, chunks=None):
        b, n = where[key]
        w = HN // n
        o0, o1 = (A.max, A.min) if least else (A.mult, A.max)
        for c in (range(n) if chunks is None else chunks):
            d0, d1 = view("mkn" if least else "mkx", 0, w), view(b, c * w, (c + 1) * w)
            o = view(out[0], out[1] + c * w, out[1] + (c + 1) * w)
            op("v", lambda: g.vector.tensor_tensor_scan(o[0], d0[0], d1[0], 0.0, o0, o1), [d0, d1], [o])

    def own(slot, h=0):
        return ("mxw", (slot * 2 + h) * HN)

    def own_min(h=0):
        return ("mno", h * HN)

    def urep(h, slot):
        b, o = own(slot, h)
        y = view(b, o + 15, o + HN, 16)
        mms(view("p%d" % h, 0, HC), [(view("wh", 0, 128), y), (view("wl", 0, 128), y)], True, True)

    def tolist(bank, col, q, src, n, start, stop):
        b, o = src
        mms(view(bank, col, col + 8 * n),
            [(view(q, 15 - j, 143 - j), view(b, o + 16 * j + 15, o + n * HN, 256)) for j in range(16)], start, stop)

    def span_max(bank, col, src, n):
        tolist(bank, col, "qo", src, n, True, False)

    def span_min(bank, col, src, n):
        tolist(bank, col, "qn", src, n, False, True)

    def low3(slot):
        tolist("p7", slot * 16, "q7", own(slot), 2, True, True)

    def ptab(k, least):
        return ("pmn" if least else "pmx", (k % 2) * 2 * HN)

    def pscan(k, h, least):
        b, o = ptab(k, least)
        scan("P%d%d" % (k, h), (b, o + h * HN), least)

    def proposal(t, h, slot):
        ua, ub, uc, ud = (view("%s%d" % (k, h), 0, HC) for k in ("ua", "ub", "uc", "ud"))
        cp(ua, view("p%d" % h, 0, HC))
        ts(ub, ua, 4095, A.bitwise_and)
        tt(uc, ub, names(t, slot, h), A.mult)
        tt(ud, uc, view("p2", h * HC, (h + 1) * HC), A.add)
        ts(names(t, slot + 1, h), ud, 6, A.arith_shift_right, 2047, A.bitwise_and)

    es, en, ths, h0, de, dq, z, d0, e0, esa, th1, q1, w1, thb, hq, m2, h1, eq, du = (
        small(n, 16) for n in ("es", "en", "ths", "h0", "de", "dq", "z", "d0", "e0", "esa", "th1", "q1", "w1", "thb", "hq", "m2", "h1",
                               "eq", "du"))
    ui, u7 = small("ui", 48, "smi"), small("u7", 48, "smi")
    kn, ki, kk = small("kn", 1), small("ki", 1, "smi"), small("kk", 1, "smi")

    def slack(t, j):
        return view("al", (t * 2 + j) * 16, (t * 2 + j) * 16 + 16)

    def second(t, h):
        h8, q8, so = sub(h0, 8 * h, 8), sub(hq, 8 * h, 8), view("so", 8 * h, 8 * h + 8)
        tt(h8, view("p3", 8 * h, 8 * h + 8), sub(ths, 8 * h, 8), A.is_le)
        tt(q8, sub(inq, 8 * h, 8), h8, A.subtract)
        ts(so, q8, float(NC), A.mult)
        cp(lists(t, 2, h), ind(view("nw%d" % (t % 2), 0, 4 * NC), so))
        send_list(t, 2, h)

    for t in range(R):
        cur, new = "tab%d" % (t % 2), "tab%d" % ((t + 1) % 2)
        gather("L00", t, lists(t, 0, 0), 2)
        gather("L01", t, lists(t, 0, 1))
        if t:
            cp(names(t, 0), lists(t, 0))
            op("v", lambda: g.vector.tensor_reduce(kn[0], T.p7[:, 64:80], AxisListType.X, A.add), [view("p7", 64, 80)], [kn])
            ts(ki, kn, -1.0, A.mult, float(8 * NC), A.add)
            ts(kk, ki, 31, A.bitwise_and)
            tt(c0, k613, kk, A.add)
        ts(view("p2", 0, NC), names(t, 0), c0, A.add, 64.0, A.mult)
        scan("L00", own(0, 0), False, [0])
        scan("L00", own_min(0), True, [0])
        scan("L00", own(0, 0), False, [1])
        urep(0, 0)
        scan("L00", own_min(0), True, [1])
        proposal(t, 0, 0)
        cp(lists(t, 1, 0), names(t, 1, 0))
        send_list(t, 1, 0)
        gather("P00", t, lists(t, 0, 0, "inl"))
        gather("L10", t, lists(t, 1, 0))
        scan("L01", own(0, 1), False)
        urep(1, 0)
        span_max("p4", 0, own(0), 2)
        scan("L01", own_min(1), True)
        span_min("p4", 0, own_min(), 2)
        proposal(t, 1, 0)
        cp(lists(t, 1, 1), names(t, 1, 1))
        send_list(t, 1, 1)
        if t == 0:
            dma("y", "dx1", T[new][:], T.xt[:], [names(t, 1, 1)], [view(new, 0, 2048)])
            cp(view("al", 0, 128), view("p7", 0, 128))
        else:
            dma("y", "dc%d" % (t - 1), T[new][:], T[cur][:], [view(cur, 0, 2048), names(t, 1, 1)], [view(new, 0, 2048)])
        gather("L11", t, lists(t, 1, 1))
        gather("P01", t, lists(t, 0, 1, "inl"))
        nx = view("nx", 0, NC)
        ts(nx, names(t, 1), 77.0, A.add)
        ts(names(t, 3), nx, 2047, A.bitwise_and)
        ts(view("p2", 0, NC), nx, c0, A.add, 64.0, A.mult)
        pscan(0, 0, False)
        pscan(0, 0, True)
        cp(es, view("p4", 0, 16))
        tt(ths, es, slack(t, 0), A.add)
        low3(0)
        for h in range(2):
            k = "L1%d" % h
            if h == 0:
                scan(k, own(1, h), False)
            urep(h, 1)
            span_max("p3", 8 * h, own(1, h), 1)
            scan(k, own_min(h), True)
            span_min("p3", 8 * h, own_min(h), 1)
            proposal(t, h, 1)
            if h == 0:
                scan("L11", own(1, 1), False)
            else:
                pscan(0, 1, False)
            second(t, h)
            gather("P1%d" % h, t, lists(t, 1, h, "inl"))
        low3(1)
        span_max("p6", 0, ptab(0, False), 2)
        pscan(0, 1, True)
        span_min("p6", 0, ptab(0, True), 2)
        pscan(1, 0, False)
        pscan(1, 0, True)
        gather("P20", t, lists(t, 2, 0, "inl"))
        gather("P21", t, lists(t, 2, 1, "inl"))
        tt(de, view("p3", 0, 16), es, A.subtract)
        tt(esa, es, slack(t, 1), A.add)
        tt(q1, h0, de, A.mult)
        tt(th1, esa, q1, A.add)
        cp(sub(ui, 0, 32), view("p7", 0, 32))
        ts(sub(u7, 0, 32), sub(ui, 0, 32), 7, A.bitwise_and)
        tt(du, sub(u7, 16, 16), sub(u7, 0, 16), A.subtract)
        if t == R - 1:
            ts(sub(iv, 8, 8), sub(iv, 8, 8), -1024.0, A.add)
        tt(sub(ib, 32, 16), iv, sub(u7, 0, 16), A.add)
        ts(sub(cb, 0, 16), hq, float(NC), A.mult)
        pscan(1, 1, False)
        span_max("p6", 16, ptab(1, False), 2)
        pscan(1, 1, True)
        span_min("p6", 16, ptab(1, True), 2)
        gather("L20", t, lists(t, 2, 0), 2)
        gather("L21", t, lists(t, 2, 1), 2)
        pscan(2, 0, False)
        cp(view("ro", t * 48, t * 48 + 32), view("p6", 0, 32))
        send_spans(t, 0)
        pscan(2, 0, True)
        pscan(2, 1, False)
        span_max("p6", 32, ptab(2, False), 2)
        pscan(2, 1, True)
        span_min("p6", 32, ptab(2, True), 2)
        scan("L20", own(2, 0), False)
        span_max("p5", 0, own(2, 0), 1)
        cp(view("ro", t * 48 + 32, t * 48 + 48), view("p6", 32, 48))
        send_spans(t, 1)
        scan("L20", own_min(0), True)
        span_min("p5", 0, own_min(0), 1)
        scan("L21", own(2, 1), False)
        low3(2)
        scan("L21", own(3), True)
        tolist("p5", 8, "qo", own(2, 1), 2, True, True)
        qs, qn, qx = (view("rin", t * 48 + 16 * k, t * 48 + 16 * k + 16) for k in range(3))
        tt(dq, qn, qs, A.subtract)
        tt(z, de, dq, A.add)
        tt(d0, z, slack(t, 0), A.is_le)
        tt(w1, esa, qs, A.add)
        tt(q1, h0, z, A.mult)
        tt(e0, h0, d0, A.is_equal)
        ts(sub(tmp, 0, 16), d0, float(NC), A.mult)
        ts(sub(tmp, 16, 16), d0, float(2 * HN), A.mult)
        tt(sub(tmp, 32, 16), d0, du, A.mult)
        tt(w1, w1, q1, A.add)
        ts(thb, e0, 65536.0, A.mult, -65536.0, A.add)
        tt(base, tmp, ib, A.add)
        tt(w1, w1, thb, A.add)
        tt(sub(d2, 0, 32), sub(cb, 0, 32), sub(base, 0, 32), A.subtract)
        cp(sub(ui, 32, 16), view("p7", 32, 48))
        ts(sub(u7, 32, 16), sub(ui, 32, 16), 7, A.bitwise_and)
        tt(sub(cb, 32, 16), iv, sub(u7, 32, 16), A.add)
        tt(sub(d2, 32, 16), sub(cb, 32, 16), sub(base, 32, 16), A.subtract)
        tt(thb, w1, qx, A.subtract)
        tt(sub(m2, 0, 8), view("p5", 0, 8), sub(thb, 0, 8), A.is_le)
        tt(sub(z, 0, 8), view("p5", 8, 16), sub(thb, 8, 8), A.subtract)
        tt(sub(m2, 8, 8), view("p5", 16, 24), sub(z, 0, 8), A.is_ge)
        for k in range(3):
            tt(sub(tmp, 16 * k, 16), m2, sub(d2, 16 * k, 16), A.mult)
        tt(fl, tmp, base, A.add)
        cp(view("fo", 0, 48), fl)
        fy, xs, xh = view("fy", 0, NC), view("xs", 0, NC), view("xh", 0, NC)
        src = ind(view("mxw", 0, 6 * HN), view("fo", 16, 32))
        op("s", lambda: g.scalar.activation(fy[0], src[0], F.Copy), [src], [fy])
        picked = ind(view("nw%d" % (t % 2), 0, 4 * NC), view("fo", 0, 16))
        vo = view("fo", 32, 48)
        if t < R - 1:
            cp(lists(t + 1, 0), picked)
            send_list(t + 1, 0)
        else:
            cp(view("ycf", 0, NC), picked)
            dma("y", "dyc", T.yc[:], T.ycf[:], [view("ycf", 0, NC)], [])
        parts = [(0, 1)] if t < R - 1 else [(0, 2), (1, 2)]
        for i, n in parts:
            w = NC // n
            xi, hi, oi = sub(xs, i * w, w), sub(xh, i * w, w), sub(vo, i * w // 16, w // 16)
            tt(xi, ind(view(cur, i * 8 * w, (i + 1) * 8 * w), oi), sub(fy, i * w, w), A.add)
            ts(hi, xi, 1, A.arith_shift_right)
            col = view(new, i * 8 * w, (i + 1) * 8 * w)
            out = ind(col, oi)
            op("v", lambda: g.vector.tensor_copy(out[0], hi[0]), [hi, oi], [col])
            if n == 2:
                dma("ys"[i], "dyx%d" % i, T.yx[:, col[2]:col[3]], col[0], [col], [])
        if t < R - 1:
            tt(sub(h1, 0, 8), view("p5", 0, 8), sub(th1, 0, 8), A.is_le)
            tt(sub(z, 8, 8), view("p5", 8, 16), sub(th1, 8, 8), A.subtract)
            tt(sub(h1, 8, 8), view("p5", 16, 24), sub(z, 8, 8), A.is_ge)
            tt(eq, h1, m2, A.is_equal)
            tt(view("rt", 0, 16), eq, e0, A.mult)
            mms(view("p7", 64, 80), [(view("ones", 0, 128), view("rt", 0, 16))], True, True)

    for q in "vstg":
        g.wait_ge(T.sem["q" + q], count[q])
    for s in DMAS:
        g.wait_ge(T.sem[s], 16)
    g.wait_ge(T.sem.loc, nloc[0])
